import numpy as np
CORES = [66,74,82,90,194,202,210,218]
N = 8
B, TIMES = 128, 3
def setup_inputs(rng):
    return {"x": (rng.standard_normal((N, 128, B), dtype=np.float32) * (0.5 + np.abs(rng.standard_normal((1, 1, B), dtype=np.float32))) / np.float32(np.sqrt(128 * N))), "a": (rng.standard_normal((N, 128, N * 128), dtype=np.float32) / 8)}
def reference(x, a):
    X, A = x.astype(np.float64), a.astype(np.float64)
    h = X
    for _ in range(TIMES):
        h = np.stack([sum(A[r][:, 128 * j:128 * j + 128].T @ h[j] for j in range(N)) for r in range(N)])
        h = h / np.sqrt((h ** 2).sum(axis=(0, 1)))
        h = h + X
    return {"y": h.astype(np.float32)}

from concourse.bass import DstId, RemoteDMATransfer
from concourse.mybir import AluOpType, AxisListType, ActivationFunctionType

N = 8
B = 128
NDIRECT = [4, 4, 4, 7]
NEV = 90

SCRATCH = {
    "A": ("sbuf", [128, N * B], "float32"),
    "X": ("sbuf", [128, N * B], "float32"),
    "V1": ("sbuf", [128, N * B], "float32"),
    "V2": ("sbuf", [128, N * B], "float32"),
    "GL": ("sbuf", [128, N * 4], "float32"),
    "SQ1": ("sbuf", [128, N * B], "float32"),
    "SQ2": ("sbuf", [128, N * B], "float32"),
    "PR": ("sbuf", [128, N * B], "float32"),
    "Q": ("sbuf", [128, 3 * B], "float32"),
    "ONES": ("sbuf", [128, B], "float32"),
    "IDN": ("sbuf", [128, B], "float32"),
    "TW": ("sbuf", [128, 4], "float32"),
    "IO": ("sbuf", [128, 32], "float32"),
    "MK": ("sbuf", [128, 96], "float32"),
    "WK": ("sbuf", [128, 192], "float32"),
    "CL": ("sbuf", [128, 32], "float32"),
    "DG": ("sbuf", [128, 3 * B], "float32"),
    "D1S": ("sbuf", [128, B], "float32"),
    "WA": ("sbuf", [128, B], "float32"),
    "WB": ("sbuf", [128, B], "float32"),
    "UA": ("sbuf", [128, B], "float32"),
    "U3": ("sbuf", [128, B], "float32"),
    "YA": ("sbuf", [128, B], "float32"),
    "Y": ("sbuf", [128, B], "float32"),
    "PA": ("psum", [128, 512], "float32"),
    "PB": ("psum", [128, 512], "float32"),
    "PC": ("psum", [128, 512], "float32"),
    "PS1": ("psum", [128, 512], "float32"),
    "PS2": ("psum", [128, 512], "float32"),
    "PG": ("psum", [128, 512], "float32"),
    "PD1": ("psum", [128, 512], "float32"),
    "PD2": ("psum", [128, 512], "float32"),
}
SEMAPHORES = (["e%d" % i for i in range(NEV)] + ["a%d_%d" % (p, j) for p in range(4) for j in range(N)]
              + ["h%d" % p for p in range(4)] + ["snt", "ldx", "lda", "sty"])


def _bits(m):
    return bin(m).count("1")


def _plan(i, p, cores, topo):
    peers = sorted([j for j in range(N) if j != i], key=lambda j: i ^ j)
    mate = [j for j in peers if topo.mates(cores[i], cores[j])]
    plane = [j for j in peers if topo.same_plane(cores[i], cores[j])]
    other = [j for j in peers if j not in mate and j not in plane]
    full = []
    a, b = list(plane), mate + other
    while a or b:
        if a:
            full.append(a.pop(0))
        if b:
            full.append(b.pop(0))
    return full[:NDIRECT[p]], full[NDIRECT[p]:]


def _helper(i, cores, topo):
    rc = cores[i]
    hosts = 1 + max(topo.host(c) for c in cores)
    for c in range(hosts * topo.CORES_PER_HOST):
        if (topo.host(c) == topo.host(rc) and topo.chip(c) == topo.chip(rc) and topo.die(c) != topo.die(rc)
                and all(topo.may_write(c, cores[j]) for j in range(N) if j != i)):
            return c
    return None


def _slot(T, p, j):
    if p == 3:
        return T.GL[:, 4 * j:4 * j + 4]
    return T[("X", "V1", "V2")[p]][:, B * j:B * j + B]


def _spread(core, i, p, dests, T, topo):
    cores = T.cores
    m = topo.mask(core, cores[dests[0]])
    for j in dests:
        m &= topo.mask(core, cores[j])
    ids = []
    for j in dests:
        rid, pid = topo.addr(cores[j], core)
        ids.append(DstId(rid=rid, pnc=pid))
    return RemoteDMATransfer(dst_ids=ids, dma_engine_mask=m, remote_sem=T.sem["a%d_%d" % (p, i)],
                             srcs=[_slot(T, p, i)], dsts=[_slot(T, p, i) for _ in dests], alu_op=0), _bits(m)


def _helper_program(g, core, i, T, topo):
    sent = 0
    for p in range(4):
        _, relay = _plan(i, p, T.cores, topo)
        if not relay:
            continue
        on = topo.mask(T.cores[i], core) & ~topo.mask(T.cores[i], T.cores[relay[0]])
        g.wait_ge(T.sem["h%d" % p], _bits(on))
        tr, n = _spread(core, i, p, relay, T, topo)
        g.remote_dma_fused([tr], local_sem=T.sem.snt)
        sent += n
    if sent:
        g.wait_ge(T.sem.snt, sent)


def rank_program(g, core, T, topo):
    cores = T.cores
    r = T.rank_of(core)
    if r is None:
        for i in range(N):
            if _helper(i, cores, topo) == core:
                _helper_program(g, core, i, T, topo)
        return

    MUL, ADD, EQ = AluOpType.mult, AluOpType.add, AluOpType.is_equal
    AF = ActivationFunctionType
    pe, dve, act, sy = g.tensor, g.vector, g.scalar, g.sync
    qn = {0: g, 1: pe, 2: dve, 3: act, 4: sy}
    G, PE, DVE, ACT, SY = 0, 1, 2, 3, 4
    nev = [0]
    seen = {}

    def new_ev(count=1):
        name = "e%d" % nev[0]
        nev[0] += 1
        return (name, count)

    def wait(q, *evs):
        for name, count in evs:
            if seen.get((q, name), 0) < count:
                qn[q].wait_ge(T.sem[name], count)
                seen[(q, name)] = count

    def done(inst):
        ev = new_ev()
        inst.then_inc(T.sem[ev[0]], 1)
        return ev

    def sl(j):
        return slice(B * j, B * j + B)

    helper = _helper(r, cores, topo)
    order, arr = [], []
    for p in range(4):
        key = {}
        cnt = {}
        for j in range(N):
            if j == r:
                continue
            d, rl = _plan(j, p, cores, topo)
            if r in d:
                key[j] = (0, d.index(r))
                src, lst = cores[j], d
            else:
                key[j] = (1, rl.index(r))
                src, lst = _helper(j, cores, topo), rl
            m = topo.mask(src, cores[lst[0]])
            for k in lst:
                m &= topo.mask(src, cores[k])
            cnt[j] = _bits(m)
        order.append(sorted(key, key=lambda j: key[j]))
        arr.append({j: ("a%d_%d" % (p, j), cnt[j]) for j in key})
    sent = [0]

    def send(p):
        direct, relay = _plan(r, p, cores, topo)
        trs = []
        if relay:
            on = topo.mask(core, helper) & ~topo.mask(core, cores[relay[0]])
            rid, pid = topo.addr(helper, core)
            trs.append(RemoteDMATransfer(dst_ids=[DstId(rid=rid, pnc=pid)], dma_engine_mask=on,
                                         remote_sem=T.sem["h%d" % p], srcs=[_slot(T, p, r)], dsts=[_slot(T, p, r)],
                                         alu_op=0))
            sent[0] += _bits(on)
        tr, n = _spread(core, r, p, direct, T, topo)
        trs.append(tr)
        sent[0] += n
        g.remote_dma_fused(trs, local_sem=T.sem.snt)

    LDX, LDA = ("ldx", 16), ("lda", 16)
    sy.dma_start(T.X[:, sl(r)], T.x[:]).then_inc(T.sem.ldx, 16)
    sy.dma_start(T.A[:], T.a[:]).then_inc(T.sem.lda, 16)
    e_ones = done(dve.memset(T.ONES[:], 1.0))
    e_tw = done(dve.memset(T.TW[:], 2.0))
    e_pad = done(dve.memset(T.GL[:, 4 * r + 3:4 * r + 4], 0.0))
    wait(G, e_ones)
    e_idn = done(g.affine_select(T.IDN[:], T.ONES[:], [[-1, B]], EQ, 0.0, 0, 1))
    e_io = done(g.iota(T.IO[:], [[0, 8], [1, 4]], 0, 0, allow_small_or_imprecise_dtypes=True))
    wait(DVE, e_io)
    e_mk = [done(dve.tensor_scalar(T.MK[:, 32 * c:32 * c + 32], T.IO[:], float(c), None, EQ)) for c in range(3)]

    wait(G, LDX)
    send(0)

    def chain(p, src, own_ev, out):
        js = [r] + order[p]
        inst = None
        for n, j in enumerate(js):
            wait(PE, own_ev if j == r else arr[p][j])
            inst = pe.matmul(out, T.A[:, sl(j)], src[:, sl(j)], n == 0, n == N - 1)
        return done(inst)

    wait(PE, LDA)
    e_p1 = chain(0, T.X, LDX, T.PA[:, 0:B])
    wait(DVE, e_p1)
    e_v1 = done(dve.tensor_copy(T.V1[:, sl(r)], T.PA[:, 0:B]))
    wait(G, e_v1)
    send(1)

    e_p2 = chain(1, T.V1, e_v1, T.PB[:, 0:B])
    e_sq1 = new_ev(N)
    for j in [r] + order[1]:
        wait(ACT, e_v1 if j == r else arr[1][j])
        act.activation(T.SQ1[:, sl(j)], T.V1[:, sl(j)], AF.Square).then_inc(T.sem[e_sq1[0]], 1)
    wait(DVE, e_p2)
    e_v2 = done(dve.tensor_copy(T.V2[:, sl(r)], T.PB[:, 0:B]))
    wait(G, e_v2)
    send(2)

    def colsum(out, src, rhs):
        inst = None
        for j in range(N):
            inst = pe.matmul(out, src[:, sl(j)], rhs, j == 0, j == N - 1)
        return done(inst)

    def col(k):
        return T.CL[:, k:k + 1]
    S11, N1, D1, S22, S21, TA, S2, N2, D2, EE, TC, C0, R3, N3, D3 = [col(k) for k in range(15)]

    wait(PE, e_sq1, e_ones)
    e_s11p = colsum(T.PS1[:, 0:1], T.SQ1, T.ONES[:, 0:1])
    wait(ACT, e_s11p)
    e_n1 = done(act.activation(N1, T.PS1[:, 0:1], AF.Sqrt))
    wait(DVE, e_n1)
    e_d1 = done(dve.reciprocal(D1, N1))
    e_s11 = done(dve.tensor_copy(S11, T.PS1[:, 0:1]))
    wait(DVE, e_d1, e_idn)
    e_dg1 = done(dve.tensor_scalar(T.DG[:, 0:B], T.IDN[:], D1, None, MUL))

    e_p3 = chain(2, T.V2, e_v2, T.PC[:, 0:B])
    e_sq2, e_pr = new_ev(N), new_ev(N)
    for j in [r] + order[2]:
        wait(ACT, e_v2 if j == r else arr[2][j])
        act.activation(T.SQ2[:, sl(j)], T.V2[:, sl(j)], AF.Square).then_inc(T.sem[e_sq2[0]], 1)
        if j == r:
            wait(DVE, e_v2, e_v1)
        else:
            wait(DVE, arr[2][j], arr[1][j])
        dve.tensor_tensor(T.PR[:, sl(j)], T.V2[:, sl(j)], T.V1[:, sl(j)], MUL).then_inc(T.sem[e_pr[0]], 1)

    wait(ACT, e_p3)
    e_q33 = done(act.activation(T.Q[:, 0:B], T.PC[:, 0:B], AF.Square))
    wait(DVE, e_p3, e_q33)
    e_q32 = done(dve.tensor_tensor(T.Q[:, B:2 * B], T.PC[:, 0:B], T.V2[:, sl(r)], MUL))
    e_q31 = done(dve.tensor_tensor(T.Q[:, 2 * B:3 * B], T.PC[:, 0:B], T.V1[:, sl(r)], MUL))
    e_g3 = new_ev(3)
    wait(PE, e_q33)
    pe.matmul(T.PG[:, 0:1], T.Q[:, 0:B], T.ONES[:, 0:1], True, True).then_inc(T.sem[e_g3[0]], 1)
    wait(PE, e_q32, e_tw)
    pe.matmul(T.PG[:, 1:2], T.Q[:, B:2 * B], T.TW[:, 0:1], True, True).then_inc(T.sem[e_g3[0]], 1)
    wait(PE, e_q31)
    pe.matmul(T.PG[:, 2:3], T.Q[:, 2 * B:3 * B], T.TW[:, 0:1], True, True).then_inc(T.sem[e_g3[0]], 1)
    wait(DVE, e_g3)
    e_gs = done(dve.tensor_copy(T.GL[:, 4 * r:4 * r + 3], T.PG[:, 0:3]))
    wait(G, e_gs, e_pad)
    send(3)

    wait(PE, e_dg1)
    e_d1b = done(pe.matmul(T.PD1[:, 0:B], T.ONES[:], T.DG[:, 0:B], True, True))
    wait(DVE, e_d1b)
    e_d1s = done(dve.tensor_copy(T.D1S[:], T.PD1[:, 0:B]))
    wait(DVE, e_d1s)
    e_wa = done(dve.tensor_tensor(T.WA[:], T.PC[:, 0:B], T.D1S[:], MUL))
    wait(DVE, e_wa)
    e_wb = done(dve.tensor_tensor(T.WB[:], T.WA[:], T.V2[:, sl(r)], ADD))
    wait(PE, e_sq2)
    e_s22p = colsum(T.PS2[:, 0:1], T.SQ2, T.ONES[:, 0:1])
    wait(PE, e_pr)
    e_s21p = colsum(T.PS2[:, 1:2], T.PR, T.TW[:, 0:1])
    wait(DVE, e_s22p, e_s21p)
    e_ss = done(dve.tensor_copy(T.CL[:, 3:5], T.PS2[:, 0:2]))
    wait(DVE, e_ss, e_s11)
    e_ta = done(dve.tensor_scalar(TA, S22, D1, S21, MUL, ADD))
    wait(DVE, e_ta)
    e_s2 = done(dve.tensor_scalar(S2, TA, D1, S11, MUL, ADD))
    wait(ACT, e_s2)
    e_n2 = done(act.activation(N2, S2, AF.Sqrt))
    wait(DVE, e_n2)
    e_d2 = done(dve.reciprocal(D2, N2))
    wait(DVE, e_d2)
    e_dg2 = done(dve.tensor_scalar(T.DG[:, B:2 * B], T.IDN[:], D2, None, MUL))
    wait(PE, e_dg2)
    e_d2b = done(pe.matmul(T.PD2[:, 0:B], T.ONES[:], T.DG[:, B:2 * B], True, True))
    e_ee = done(dve.tensor_scalar(EE, D1, D2, None, MUL))
    e_tc = done(dve.tensor_scalar(TC, S22, D2, S21, MUL, ADD))
    wait(DVE, e_ee, e_tc, *e_mk)
    e_w0 = done(dve.tensor_scalar(T.WK[:, 0:32], T.MK[:, 0:32], EE, EE, MUL, MUL))
    e_w1 = done(dve.tensor_scalar(T.WK[:, 32:64], T.MK[:, 32:64], EE, D2, MUL, MUL))
    e_w2 = done(dve.tensor_scalar(T.WK[:, 64:96], T.MK[:, 64:96], EE, None, MUL))
    e_c0 = done(dve.tensor_scalar(C0, TC, D2, S11, MUL, ADD))
    wait(DVE, e_w0, e_w1)
    e_w3 = done(dve.tensor_tensor(T.WK[:, 96:128], T.WK[:, 0:32], T.WK[:, 32:64], ADD))
    wait(DVE, e_w3, e_w2)
    e_wt = done(dve.tensor_tensor(T.WK[:, 128:160], T.WK[:, 96:128], T.WK[:, 64:96], ADD))
    wait(DVE, e_d2b, e_wb)
    e_ua = done(dve.tensor_tensor(T.UA[:], T.WB[:], T.PD2[:, 0:B], MUL))
    wait(DVE, e_ua)
    e_u3 = done(dve.tensor_tensor(T.U3[:], T.UA[:], T.V1[:, sl(r)], ADD))

    wait(DVE, e_wt, e_gs, e_pad, *[arr[3][j] for j in order[3]])
    e_mu = done(dve.tensor_tensor(T.WK[:, 160:192], T.GL[:], T.WK[:, 128:160], MUL))
    wait(DVE, e_mu)
    e_r3 = done(dve.tensor_reduce(R3, T.WK[:, 160:192], AxisListType.X, ADD))
    wait(ACT, e_r3, e_c0)
    e_n3 = done(act.activation(N3, R3, AF.Sqrt, bias=C0))
    wait(DVE, e_n3)
    e_d3 = done(dve.reciprocal(D3, N3))
    wait(DVE, e_d3)
    e_dg3 = done(dve.tensor_scalar(T.DG[:, 2 * B:3 * B], T.IDN[:], D3, None, MUL))
    wait(PE, e_dg3)
    e_d3b = done(pe.matmul(T.PA[:, 0:B], T.ONES[:], T.DG[:, 2 * B:3 * B], True, True))
    wait(DVE, e_d3b, e_u3)
    e_ya = done(dve.tensor_tensor(T.YA[:], T.U3[:], T.PA[:, 0:B], MUL))
    wait(DVE, e_ya, LDX)
    e_y = done(dve.tensor_tensor(T.Y[:], T.YA[:], T.X[:, sl(r)], ADD))
    wait(SY, e_y)
    sy.dma_start(T.y[:], T.Y[:]).then_inc(T.sem.sty, 16)
    sy.wait_ge(T.sem.sty, 16)
    g.wait_ge(T.sem.snt, sent[0])
